import numpy as np
import ml_dtypes


def mxq(x, axis, fmt="e4m3"):
    dtype, down = {"e4m3": (ml_dtypes.float8_e4m3fn, 7), "e5m2": (ml_dtypes.float8_e5m2, 14)}[fmt]
    v = np.moveaxis(np.asarray(x, np.float32).astype(ml_dtypes.bfloat16).astype(np.float64), axis, -1)
    blocks = v.reshape(v.shape[:-1] + (-1, 32))
    amax = np.abs(blocks).max(-1, keepdims=True)
    byte = np.maximum(np.where(amax > 0, np.frexp(amax)[1] - 1 + 127, 0) - down, 1)
    scale = np.exp2(byte - 127.0)
    codes = (blocks / scale).astype(np.float32).astype(dtype).astype(np.float64)
    return np.moveaxis((codes * scale).reshape(v.shape), -1, axis)


WIDE = False


def mx_kscale(k):
    if not WIDE:
        return np.ones(k)
    levels = np.array([10, -10, 5, -5, 0])
    if k % 512:
        return np.exp2(np.random.permutation(np.resize(levels, k // 32))).repeat(32)
    a = np.empty((k // 512, 16))
    for p in range(k // 512):
        a[p, :8] = np.random.permutation(np.resize(levels, 8))
        for g in range(8):
            far = levels[np.abs(levels - a[p, g]) >= 10]
            a[p, g + 8] = far[np.random.randint(len(far))]
    return np.exp2(a.ravel()).repeat(32)


def f64(x):
    return np.asarray(x).astype(np.float64)


def striped(idx):
    return np.tile(idx.reshape(-1, 16).T, (8, 1)).astype(np.uint16)


def unstriped(offs):
    return offs[:16].T.reshape(-1).astype(np.int64)


def striped8(idx):
    return np.concatenate([x.reshape(-1, 16).T for x in idx]).astype(np.uint16)


def runs(offs, k):
    lists = np.stack([offs[16 * r : 16 * r + 16].T.reshape(-1) for r in range(8)]).astype(np.int64)
    return lists[np.arange(k) % 512 // 64]


def pack_weight(w):
    k, n = w.shape
    w = f64(np.asarray(w, np.float32).astype(ml_dtypes.bfloat16)).reshape(k // 32, 32, n)
    amax = np.abs(w).max(1)
    byte = np.clip(np.where(amax > 0, np.frexp(amax)[1] - 1 + 127 - 7, 1), 1, 254)
    scaled = (w * np.exp2(127.0 - byte)[:, None, :]).reshape(k, n).astype(np.float32)
    words = np.ascontiguousarray(scaled.reshape(k // 512, 128, 4, n).transpose(0, 1, 3, 2)).astype(ml_dtypes.float8_e4m3fn).view(np.uint8)
    return words, np.ascontiguousarray(byte.astype(np.uint8).reshape(k // 512, 16, n))


def unpack_weight(words, scales):
    g, p, n, _ = words.shape
    vals = np.ascontiguousarray(words).view(ml_dtypes.float8_e4m3fn).astype(np.float64) * np.repeat(np.exp2(scales.astype(np.float64) - 127.0), 8, axis=1)[..., None]
    return vals.transpose(0, 1, 3, 2).reshape(g * 512, n)


E2M1 = np.array([0.0, 0.5, 1.0, 1.5, 2.0, 3.0, 4.0, 6.0, -0.0, -0.5, -1.0, -1.5, -2.0, -3.0, -4.0, -6.0])


def pack_fp4(w):
    k, n = w.shape
    w = f64(np.asarray(w, np.float32).astype(ml_dtypes.bfloat16)).reshape(k // 32, 32, n)
    amax = np.abs(w).max(1)
    mant, ex = np.frexp(amax / 6.0)
    byte = np.clip(np.where(amax > 0, np.where(mant > 0.5, ex, ex - 1) + 127, 1), 1, 254)
    scaled = (w * np.exp2(127.0 - byte)[:, None, :]).reshape(k, n).astype(np.float32)
    c = np.ascontiguousarray(scaled.reshape(k // 512, 128, 4, n).transpose(0, 1, 3, 2)).astype(ml_dtypes.float4_e2m1fn).view(np.uint8) & 0xF
    words = (c[..., 0::2] | (c[..., 1::2] << 4)).reshape(k // 512, 128, 2 * n)
    return np.ascontiguousarray(words), np.ascontiguousarray(byte.astype(np.uint8).reshape(k // 512, 16, n))


def unpack_fp4(words, scales):
    g, _, n = scales.shape
    words = np.ascontiguousarray(words).reshape(g, 128, n, 2)
    nib = np.empty((g, 128, n, 4), np.uint8)
    nib[..., 0::2] = words & 0xF
    nib[..., 1::2] = words >> 4
    vals = E2M1[nib] * np.repeat(np.exp2(scales.astype(np.float64) - 127.0), 8, axis=1)[..., None]
    return vals.transpose(0, 1, 3, 2).reshape(g * 512, n)


def planes(y):
    n, m = y.shape
    v = y.astype(np.float32).astype(ml_dtypes.bfloat16).astype(np.float64).reshape(n // 32, 32, m)
    top = np.abs(v).max(1)
    byte = np.clip(np.where(top > 0, np.frexp(top)[1] - 1 + 127 - 7, 1), 1, 254)
    codes = (v * np.exp2(127.0 - byte)[:, None, :]).reshape(n, m).astype(np.float32).astype(ml_dtypes.float8_e4m3fn).view(np.uint8)
    words = codes.reshape(n // 512, 128, 4, m).transpose(0, 1, 3, 2)
    return np.ascontiguousarray(words), np.ascontiguousarray(byte.astype(np.uint8).reshape(n // 512, 16, m))


K, T, S, H, C = 512, 2048, 512, 512, 512


def setup_inputs():
    n = np.random.standard_normal
    s = mx_kscale(K)[:, None]
    packed_xT = pack_weight(n((K, T)) * s)
    packed_w1 = pack_fp4(n((K, H)) / np.sqrt(K) / s)
    return {
        "x_words": packed_xT[0],
        "x_scales": packed_xT[1],
        "w1_words": packed_w1[0],
        "w1_scales": packed_w1[1],
        "gs": (np.random.uniform(0.5, 1.5, (K, 1)) / s).astype(np.float32),
        "offs": striped(np.random.permutation(T)[:S]),
        "n1": striped8(np.stack([np.random.permutation(S) for _ in range(8)])),
        "n2": striped8(np.stack([np.random.permutation(S) for _ in range(8)])),
        "n3": striped8(np.stack([np.random.permutation(S) for _ in range(8)])),
        "n4": striped8(np.stack([np.random.permutation(S) for _ in range(8)])),
        "cand": striped(np.random.permutation(T)[:C]),
        "n5": striped8(np.stack([np.random.permutation(S) for _ in range(8)])),
        "n6": striped8(np.stack([np.random.permutation(S) for _ in range(8)])),
    }


def reference(x_words, x_scales, w1_words, w1_scales, gs, offs, n1, n2, n3, n4, cand, n5, n6):
    x_cand = unpack_weight(x_words, x_scales)[:, unstriped(cand)]
    xq = unpack_weight(x_words, x_scales)[:, unstriped(offs)]
    y = unpack_fp4(w1_words, w1_scales).T @ xq
    z = f64(gs) * (0.75 * ((y[np.arange(H)[:, None], runs(n1, H)]) * (y[np.arange(H)[:, None], runs(n2, H)]) - ((y[np.arange(H)[:, None], runs(n3, H)]) * (y[np.arange(H)[:, None], runs(n4, H)]))))
    s = 0.0625 * ((x_cand.T @ mxq(z, 0, "e4m3")))
    st = s + 0.5 * (s[np.arange(C)[:, None], runs(n5, C)])
    out_0 = st - (st[np.arange(C)[:, None], runs(n6, C)])
    return (out_0,) + planes(out_0)

@@ -1,0 +1,224 @@
+from contextlib import ExitStack
+
+import concourse.mybir as mybir
+from concourse.masks import make_identity
+
+F32 = mybir.dt.float32
+BF16 = mybir.dt.bfloat16
+I32 = mybir.dt.int32
+U32 = mybir.dt.uint32
+U16 = mybir.dt.uint16
+U8 = mybir.dt.uint8
+FP8X4 = mybir.dt.float8_e4m3fn_x4
+FP4X4 = mybir.dt.float4_e2m1fn_x4
+MULT = mybir.AluOpType.mult
+ADD = mybir.AluOpType.add
+COPY = mybir.ActivationFunctionType.Copy
+
+P = 128
+PACK = 4
+T = 2048
+S = 512
+FLOPS = 2 * 2 * 512 * 512 * 512
+
+Z_CHUNKS = ((0, 384), (384, 512))
+ST_CHUNKS = ((0, 256), (256, 512))
+OUT_CHUNKS = ((0, 256), (256, 384), (384, 512))
+
+
+def entries(lst, lo, hi):
+    return lst[:, lo // 16 : hi // 16]
+
+
+def tile_picked_canddethop_none_po_kernel(
+    tc, x_words, x_scales, w1_words, w1_scales, gs, offs, n1, n2, n3, n4, cand, n5, n6, out_0, out_1, out_2
+):
+    nc = tc.nc
+    with ExitStack() as ctx:
+        keep = ctx.enter_context(tc.tile_pool(name="keep", bufs=1))
+        psum = ctx.enter_context(tc.psum_pool(name="psum", bufs=1))
+
+        def sb(name, shape, dtype, tag=None):
+            return keep.tile(shape, dtype, name=name, tag=tag or name, align_bytes=64)
+
+        def bank(number, name, shape):
+            return psum.tile(shape, F32, name=name, tag="bank%d" % number)
+
+        w_raw = sb("w_raw", [P, 2 * S], U8)
+        xw = sb("xw", [P, T], I32)
+        xs = sb("xs", [P, T], U8)
+        ws_raw = sb("ws_raw", [P, S], U8)
+        lists = {}
+
+        def load_list(name, source):
+            lists[name] = keep.tile([P, S // 16], U16, name="list_" + name)
+            nc.sync.dma_start(lists[name][:], source)
+
+        def load_scale_rows(queue, tile, source, q):
+            queue.dma_start(tile[32 * q : 32 * q + 4, :].bitcast(I32), source[0, 4 * q : 4 * q + 4, :].bitcast(I32))
+
+        nc.vector.memset(xs[:].bitcast(I32), 0)
+        nc.gpsimd.memset(ws_raw[:].bitcast(I32), 0)
+        gain = sb("gain", [P, PACK], F32)
+        load_list("offs", offs)
+        nc.sync.dma_start(w_raw[:].bitcast(I32), w1_words[0].bitcast(I32))
+        nc.sync.dma_start(xw[:], x_words[0].rearrange("p n t -> p (n t)").bitcast(I32))
+        for q in range(4):
+            load_scale_rows(nc.sync, xs, x_scales, q)
+        for q in range(4):
+            load_scale_rows(nc.scalar if q < 3 else nc.gpsimd, ws_raw, w1_scales, q)
+        nc.gpsimd.dma_start(gain[:], gs.rearrange("(p t) o -> p (t o)", t=PACK))
+        for name, source in (("cand", cand), ("n1", n1), ("n3", n3), ("n2", n2), ("n4", n4), ("n5", n5), ("n6", n6)):
+            load_list(name, source)
+        ident = sb("ident", [P, P], F32)
+        make_identity(nc, ident[:])
+
+        gain_pos = sb("gain_pos", [P, PACK], F32)
+        gain_neg = sb("gain_neg", [P, PACK], F32)
+        nc.scalar.activation(gain_pos[:], gain[:], COPY, scale=0.75)
+        nc.scalar.activation(gain_neg[:], gain[:], COPY, scale=-0.75)
+
+        w_dealt = sb("w_dealt", [P, 2 * S], U8)
+        ws_dealt = sb("ws_dealt", [P, S], U8)
+        nc.vector.tensor_copy(
+            w_dealt[:].rearrange("p (t m b) -> p m t b", t=PACK, b=2), w_raw[:].rearrange("p (m t b) -> p m t b", t=PACK, b=2)
+        )
+        tok_w = sb("tok_w", [P, S], U32)
+        tok_s = sb("tok_s", [P, S], U8)
+        nc.vector.tensor_copy(tok_w[:], xw[:].bitcast(U32).indirect(lists["offs"][:]))
+        nc.vector.tensor_copy(tok_s[:], xs[:].indirect(lists["offs"][:]))
+        nc.vector.tensor_copy(ws_dealt[:].rearrange("p (t m) -> p m t", t=PACK), ws_raw[:].rearrange("p (m t) -> p m t", t=PACK))
+
+        cand_s = sb("cand_s", [P, S], U8)
+        cand_s_dealt = sb("cand_s_dealt", [P, S], U8)
+        nc.vector.tensor_copy(cand_s[:], xs[:].indirect(lists["cand"][:]))
+        nc.vector.tensor_copy(cand_s_dealt[:].rearrange("p (t m) -> p m t", t=PACK), cand_s[:].rearrange("p (m t) -> p m t", t=PACK))
+
+        y_pos, y_neg, y_plain = [], [], []
+        for t in range(PACK):
+            acc = bank(t, "y_acc%d" % t, [P, S])
+            nc.tensor.matmul_mx(
+                out=acc[:],
+                lhsT=w_dealt[:, 2 * P * t : 2 * P * (t + 1)].bitcast(FP4X4),
+                lhsT_scale=ws_dealt[:, P * t : P * (t + 1)],
+                rhs=tok_w[:].bitcast(FP8X4),
+                rhs_scale=tok_s[:],
+                start=True,
+                stop=True,
+            )
+            y_pos.append(sb("y_pos%d" % t, [P, S], F32))
+            y_neg.append(sb("y_neg%d" % t, [P, S], F32))
+            y_plain.append(sb("y_plain%d" % t, [P, S], F32))
+            nc.scalar.activation(y_pos[t][:], acc[:], COPY, scale=gain_pos[:, t : t + 1])
+            nc.scalar.activation(y_neg[t][:], acc[:], COPY, scale=gain_neg[:, t : t + 1])
+            nc.scalar.copy(y_plain[t][:], acc[:])
+
+        left = sb("left", [P, S], F32)
+        right = sb("right", [P, S], F32, tag="right")
+        z_words = sb("z_words", [P, S], U32)
+        z_scales = sb("z_scales", [P, S], U8)
+        z_grouped = []
+        for lo, hi in Z_CHUNKS:
+            width = hi - lo
+            blocks = range(lo // P, hi // P)
+            turned = {b: bank(4 + b, "turned%d" % b, [P, PACK, P]) for b in blocks}
+            for t in range(PACK):
+                first = sb("first%d_%d" % (lo, t), [P, width], F32)
+                second = sb("second%d_%d" % (lo, t), [P, width], F32)
+                nc.vector.tensor_copy(left[:, :width], y_pos[t][:].indirect(entries(lists["n1"], lo, hi)))
+                nc.vector.tensor_copy(right[:, :width], y_neg[t][:].indirect(entries(lists["n3"], lo, hi)))
+                nc.vector.tensor_tensor(first[:], y_plain[t][:].indirect(entries(lists["n2"], lo, hi)), left[:, :width], MULT)
+                nc.vector.tensor_tensor(second[:], y_plain[t][:].indirect(entries(lists["n4"], lo, hi)), right[:, :width], MULT)
+                for b in blocks:
+                    cols = slice(b * P - lo, (b + 1) * P - lo)
+                    nc.tensor.matmul(turned[b][:, t, :], first[:, cols], ident[:], start=True, stop=False, is_transpose=True)
+                    nc.tensor.matmul(turned[b][:, t, :], second[:, cols], ident[:], start=False, stop=True, is_transpose=True)
+            for b in blocks:
+                pairs = sb("pairs%d" % b, [P, S], BF16)
+                nc.scalar.copy(
+                    pairs[:].rearrange("j (u p e) -> j u p e", u=2, e=2), turned[b][:].rearrange("j (u e) p -> j u p e", e=2)
+                )
+                back = bank(b, "back%d" % b, [P, 2, P])
+                for u in range(2):
+                    nc.tensor.transpose(back[:, u, :], pairs[:].bitcast(F32)[:, u * P : (u + 1) * P], ident[:])
+                grouped = sb("grouped%d" % b, [P, S], BF16)
+                nc.scalar.copy(grouped[:].bitcast(F32).rearrange("p (j u) -> p j u", u=2), back[:].rearrange("p u j -> p j u"))
+                z_grouped.append(grouped)
+
+        def quantize_z(b):
+            cols = slice(b * P, (b + 1) * P)
+            nc.vector.quantize_mx(out=z_words[:, cols].bitcast(FP8X4), scales=z_scales[:, cols], in_=z_grouped[b][:])
+
+        cand_w = sb("cand_w", [P, S], U32, tag="right")
+        cand_w_dealt = sb("cand_w_dealt", [P, S], U32)
+        for b in range(3):
+            quantize_z(b)
+        nc.vector.tensor_copy(cand_w[:], xw[:].bitcast(U32).indirect(lists["cand"][:]))
+        nc.vector.tensor_copy(
+            cand_w_dealt[:].bitcast(I32).rearrange("p (t m) -> p m t", t=PACK), cand_w[:].bitcast(I32).rearrange("p (m t) -> p m t", t=PACK)
+        )
+
+        def score(acc, t, lo, hi):
+            nc.tensor.matmul_mx(
+                out=acc,
+                lhsT=cand_w_dealt[:, P * t : P * (t + 1)].bitcast(FP8X4),
+                lhsT_scale=cand_s_dealt[:, P * t : P * (t + 1)],
+                rhs=z_words[:, lo:hi].bitcast(FP8X4),
+                rhs_scale=z_scales[:, lo:hi],
+                start=True,
+                stop=True,
+            )
+
+        s_half = [sb("s_half%d" % t, [P, S], F32) for t in range(PACK)]
+        s_full = [sb("s_full%d" % t, [P, S], F32) for t in range(PACK)]
+
+        def empty(acc, t, lo, hi):
+            nc.scalar.activation(s_half[t][:, lo:hi], acc, COPY, scale=0.03125)
+            nc.scalar.activation(s_full[t][:, lo:hi], acc, COPY, scale=0.0625)
+
+        early = bank(4, "s_early", [P, 384])
+        score(early[:, 0:256], 0, 0, 256)
+        score(early[:, 256:384], 0, 256, 384)
+        empty(early[:], 0, 0, 384)
+        quantize_z(3)
+        late = bank(5, "s_late", [P, P])
+        score(late[:], 0, 384, 512)
+        empty(late[:], 0, 384, 512)
+        for t, number in ((1, 6), (2, 0), (3, 1)):
+            acc = bank(number, "s_acc%d" % t, [P, S])
+            score(acc[:], t, 0, S)
+            empty(acc[:], t, 0, S)
+
+        st, st_neg = [], []
+        for t in range(PACK):
+            st.append(sb("st%d" % t, [P, S], F32))
+            for lo, hi in ST_CHUNKS:
+                nc.vector.tensor_tensor(st[t][:, lo:hi], s_half[t][:].indirect(entries(lists["n5"], lo, hi)), s_full[t][:, lo:hi], ADD)
+        for t in range(PACK):
+            st_neg.append(sb("st_neg%d" % t, [P, S], F32))
+            nc.scalar.activation(st_neg[t][:], st[t][:], COPY, scale=-1.0)
+
+        out_rows = out_0.rearrange("(p t) j -> p t j", t=PACK)
+        o_words = sb("o_words", [P, S], U32)
+        o_scales = sb("o_scales", [P, S], U8)
+        words_out = out_1[0].rearrange("p n t -> p (n t)").bitcast(I32)
+        rounded = []
+        for lo, hi in OUT_CHUNKS:
+            width = hi - lo
+            result = sb("result%d" % lo, [P, PACK, width], F32)
+            for t in range(PACK):
+                nc.vector.tensor_tensor(result[:, t, :], st_neg[t][:].indirect(entries(lists["n6"], lo, hi)), st[t][:, lo:hi], ADD)
+            nc.sync.dma_start(out_rows[:, :, lo:hi], result[:])
+            grouped = sb("o_grouped%d" % lo, [P, width * PACK], BF16)
+            nc.scalar.copy(
+                grouped[:].rearrange("p (c i t) -> p c t i", i=4, t=PACK), result[:].rearrange("p t (c i) -> p c t i", i=4)
+            )
+            rounded.append(grouped)
+        for (lo, hi), grouped in zip(OUT_CHUNKS, rounded):
+            nc.vector.quantize_mx(out=o_words[:, lo:hi].bitcast(FP8X4), scales=o_scales[:, lo:hi], in_=grouped[:])
+            if hi >= 384:
+                start = 0 if hi == 384 else lo
+                nc.sync.dma_start(words_out[:, start:hi], o_words[:, start:hi].bitcast(I32))
+        for q in range(4):
+            queue = nc.scalar if q % 2 == 0 else nc.sync
+            queue.dma_start(out_2[0, 4 * q : 4 * q + 4, :].bitcast(I32), o_scales[32 * q : 32 * q + 4, :].bitcast(I32))

@@ -21,7 +21,6 @@ T = 2048
 S = 512
 FLOPS = 2 * 2 * 512 * 512 * 512
 
-Z_CHUNKS = ((0, 384), (384, 512))
 ST_CHUNKS = ((0, 256), (256, 512))
 OUT_CHUNKS = ((0, 256), (256, 384), (384, 512))
 
@@ -57,17 +56,17 @@ def tile_picked_canddethop_none_po_kernel(
         def load_scale_rows(queue, tile, source, q):
             queue.dma_start(tile[32 * q : 32 * q + 4, :].bitcast(I32), source[0, 4 * q : 4 * q + 4, :].bitcast(I32))
 
-        nc.vector.memset(xs[:].bitcast(I32), 0)
+        nc.gpsimd.memset(xs[:].bitcast(I32), 0)
         nc.gpsimd.memset(ws_raw[:].bitcast(I32), 0)
         gain = sb("gain", [P, PACK], F32)
         load_list("offs", offs)
         nc.sync.dma_start(w_raw[:].bitcast(I32), w1_words[0].bitcast(I32))
+        for q in range(4):
+            load_scale_rows(nc.sync if q < 2 else nc.scalar, xs, x_scales, q)
         nc.sync.dma_start(xw[:], x_words[0].rearrange("p n t -> p (n t)").bitcast(I32))
         for q in range(4):
-            load_scale_rows(nc.sync, xs, x_scales, q)
-        for q in range(4):
-            load_scale_rows(nc.scalar if q < 3 else nc.gpsimd, ws_raw, w1_scales, q)
-        nc.gpsimd.dma_start(gain[:], gs.rearrange("(p t) o -> p (t o)", t=PACK))
+            load_scale_rows(nc.sync, ws_raw, w1_scales, q)
+        nc.sync.dma_start(gain[:], gs.rearrange("(p t) o -> p (t o)", t=PACK))
         for name, source in (("cand", cand), ("n1", n1), ("n3", n3), ("n2", n2), ("n4", n4), ("n5", n5), ("n6", n6)):
             load_list(name, source)
         ident = sb("ident", [P, P], F32)
@@ -85,14 +84,16 @@ def tile_picked_canddethop_none_po_kernel(
         )
         tok_w = sb("tok_w", [P, S], U32)
         tok_s = sb("tok_s", [P, S], U8)
-        nc.vector.tensor_copy(tok_w[:], xw[:].bitcast(U32).indirect(lists["offs"][:]))
+        ws_from = ws_raw[:].rearrange("p (m t) -> p m t", t=PACK)
+        ws_to = ws_dealt[:].rearrange("p (t m) -> p m t", t=PACK)
         nc.vector.tensor_copy(tok_s[:], xs[:].indirect(lists["offs"][:]))
-        nc.vector.tensor_copy(ws_dealt[:].rearrange("p (t m) -> p m t", t=PACK), ws_raw[:].rearrange("p (m t) -> p m t", t=PACK))
+        nc.vector.tensor_copy(tok_w[:], xw[:].bitcast(U32).indirect(lists["offs"][:]))
+        nc.vector.tensor_copy(ws_to[:, :, 0], ws_from[:, :, 0])
 
-        cand_s = sb("cand_s", [P, S], U8)
-        cand_s_dealt = sb("cand_s_dealt", [P, S], U8)
-        nc.vector.tensor_copy(cand_s[:], xs[:].indirect(lists["cand"][:]))
-        nc.vector.tensor_copy(cand_s_dealt[:].rearrange("p (t m) -> p m t", t=PACK), cand_s[:].rearrange("p (m t) -> p m t", t=PACK))
+        nc.vector.tensor_copy(ws_to[:, :, 1:], ws_from[:, :, 1:])
+        cand_w = sb("cand_w", [P, S], U32)
+        cand_w_dealt = sb("cand_w_dealt", [P, S], U32)
+        nc.vector.tensor_copy(cand_w[:], xw[:].bitcast(U32).indirect(lists["cand"][:]))
 
         y_pos, y_neg, y_plain = [], [], []
         for t in range(PACK):
@@ -113,56 +114,82 @@ def tile_picked_canddethop_none_po_kernel(
             nc.scalar.activation(y_neg[t][:], acc[:], COPY, scale=gain_neg[:, t : t + 1])
             nc.scalar.copy(y_plain[t][:], acc[:])
 
-        left = sb("left", [P, S], F32)
-        right = sb("right", [P, S], F32, tag="right")
+        EARLY = 3 * P
+        left = sb("left", [P, EARLY], F32)
+        right = sb("right", [P, EARLY], F32)
         z_words = sb("z_words", [P, S], U32)
         z_scales = sb("z_scales", [P, S], U8)
-        z_grouped = []
-        for lo, hi in Z_CHUNKS:
-            width = hi - lo
-            blocks = range(lo // P, hi // P)
-            turned = {b: bank(4 + b, "turned%d" % b, [P, PACK, P]) for b in blocks}
-            for t in range(PACK):
-                first = sb("first%d_%d" % (lo, t), [P, width], F32)
-                second = sb("second%d_%d" % (lo, t), [P, width], F32)
-                nc.vector.tensor_copy(left[:, :width], y_pos[t][:].indirect(entries(lists["n1"], lo, hi)))
-                nc.vector.tensor_copy(right[:, :width], y_neg[t][:].indirect(entries(lists["n3"], lo, hi)))
-                nc.vector.tensor_tensor(first[:], y_plain[t][:].indirect(entries(lists["n2"], lo, hi)), left[:, :width], MULT)
-                nc.vector.tensor_tensor(second[:], y_plain[t][:].indirect(entries(lists["n4"], lo, hi)), right[:, :width], MULT)
-                for b in blocks:
-                    cols = slice(b * P - lo, (b + 1) * P - lo)
-                    nc.tensor.matmul(turned[b][:, t, :], first[:, cols], ident[:], start=True, stop=False, is_transpose=True)
-                    nc.tensor.matmul(turned[b][:, t, :], second[:, cols], ident[:], start=False, stop=True, is_transpose=True)
-            for b in blocks:
-                pairs = sb("pairs%d" % b, [P, S], BF16)
-                nc.scalar.copy(
-                    pairs[:].rearrange("j (u p e) -> j u p e", u=2, e=2), turned[b][:].rearrange("j (u e) p -> j u p e", e=2)
-                )
-                back = bank(b, "back%d" % b, [P, 2, P])
-                for u in range(2):
-                    nc.tensor.transpose(back[:, u, :], pairs[:].bitcast(F32)[:, u * P : (u + 1) * P], ident[:])
-                grouped = sb("grouped%d" % b, [P, S], BF16)
-                nc.scalar.copy(grouped[:].bitcast(F32).rearrange("p (j u) -> p j u", u=2), back[:].rearrange("p u j -> p j u"))
-                z_grouped.append(grouped)
 
-        def quantize_z(b):
+        def fetch(t, lo, hi, into):
+            nc.vector.tensor_copy(into[:, : hi - lo], y_pos[t][:].indirect(entries(lists["n1"], lo, hi)))
+            nc.vector.tensor_copy(right[:, : hi - lo], y_neg[t][:].indirect(entries(lists["n3"], lo, hi)))
+
+        def multiply(t, lo, hi, fetched, first, second):
+            nc.vector.tensor_tensor(first, y_plain[t][:].indirect(entries(lists["n2"], lo, hi)), fetched[:, : hi - lo], MULT)
+            nc.vector.tensor_tensor(second, y_plain[t][:].indirect(entries(lists["n4"], lo, hi)), right[:, : hi - lo], MULT)
+
+        def quantize_z(b, grouped):
             cols = slice(b * P, (b + 1) * P)
-            nc.vector.quantize_mx(out=z_words[:, cols].bitcast(FP8X4), scales=z_scales[:, cols], in_=z_grouped[b][:])
+            nc.vector.quantize_mx(out=z_words[:, cols].bitcast(FP8X4), scales=z_scales[:, cols], in_=grouped[:])
 
-        cand_w = sb("cand_w", [P, S], U32, tag="right")
-        cand_w_dealt = sb("cand_w_dealt", [P, S], U32)
+        turned = [bank(4 + b, "turned%d" % b, [P, PACK, P]) for b in range(3)]
+        for t in range(PACK):
+            first = sb("first%d" % t, [P, EARLY], F32)
+            second = sb("second%d" % t, [P, EARLY], F32)
+            fetch(t, 0, EARLY, left)
+            if t == 0:
+                nc.vector.tensor_copy(
+                    cand_w_dealt[:].bitcast(I32).rearrange("p (t m) -> p m t", t=PACK),
+                    cand_w[:].bitcast(I32).rearrange("p (m t) -> p m t", t=PACK),
+                )
+            multiply(t, 0, EARLY, left, first[:], second[:])
+            for b in range(3):
+                cols = slice(b * P, (b + 1) * P)
+                nc.tensor.matmul(turned[b][:, t, :], first[:, cols], ident[:], start=True, stop=False, is_transpose=True)
+                nc.tensor.matmul(turned[b][:, t, :], second[:, cols], ident[:], start=False, stop=True, is_transpose=True)
+        z_grouped = []
         for b in range(3):
-            quantize_z(b)
-        nc.vector.tensor_copy(cand_w[:], xw[:].bitcast(U32).indirect(lists["cand"][:]))
-        nc.vector.tensor_copy(
-            cand_w_dealt[:].bitcast(I32).rearrange("p (t m) -> p m t", t=PACK), cand_w[:].bitcast(I32).rearrange("p (m t) -> p m t", t=PACK)
+            pairs = sb("pairs%d" % b, [P, S], BF16)
+            nc.scalar.copy(
+                pairs[:].rearrange("j (u p e) -> j u p e", u=2, e=2), turned[b][:].rearrange("j (u e) p -> j u p e", e=2)
+            )
+            back = bank(b, "back%d" % b, [P, 2, P])
+            for u in range(2):
+                nc.tensor.transpose(back[:, u, :], pairs[:].bitcast(F32)[:, u * P : (u + 1) * P], ident[:])
+            z_grouped.append(sb("grouped%d" % b, [P, S], BF16))
+            nc.scalar.copy(z_grouped[b][:].bitcast(F32).rearrange("p (j u) -> p j u", u=2), back[:].rearrange("p u j -> p j u"))
+
+        first = sb("first_late", [P, PACK, P], F32)
+        second = sb("second_late", [P, PACK, P], F32)
+        for t in range(PACK - 1):
+            fetch(t, EARLY, S, left)
+            multiply(t, EARLY, S, left, first[:, t, :], second[:, t, :])
+        cand_s = sb("cand_s", [P, S], U8, tag="y_plain2")
+        cs_from = cand_s[:].rearrange("p (m t) -> p m t", t=PACK)
+        cs_first = sb("cs_first", [P, P], U8)
+        nc.vector.tensor_copy(cand_s[:], xs[:].indirect(lists["cand"][:]))
+        for b in range(3):
+            quantize_z(b, z_grouped[b])
+        nc.vector.tensor_copy(cs_first[:], cs_from[:, :, 0])
+        left_last = sb("left_last", [P, P], F32, tag="grouped2")
+        fetch(PACK - 1, EARLY, S, left_last)
+        multiply(PACK - 1, EARLY, S, left_last, first[:, PACK - 1, :], second[:, PACK - 1, :])
+        grouped_late = sb("grouped3", [P, S], BF16)
+        nc.vector.tensor_tensor(
+            grouped_late[:].rearrange("p (c i t) -> p c t i", i=4, t=PACK),
+            first[:].rearrange("p t (c i) -> p c t i", i=4),
+            second[:].rearrange("p t (c i) -> p c t i", i=4),
+            ADD,
         )
+        quantize_z(3, grouped_late)
+        cs_rest = sb("cs_rest", [P, 3 * P], U8, tag="grouped3")
+        nc.vector.tensor_copy(cs_rest[:].rearrange("p (t m) -> p m t", t=3), cs_from[:, :, 1:])
 
         def score(acc, t, lo, hi):
             nc.tensor.matmul_mx(
                 out=acc,
                 lhsT=cand_w_dealt[:, P * t : P * (t + 1)].bitcast(FP8X4),
-                lhsT_scale=cand_s_dealt[:, P * t : P * (t + 1)],
+                lhsT_scale=cs_first[:] if t == 0 else cs_rest[:, P * (t - 1) : P * t],
                 rhs=z_words[:, lo:hi].bitcast(FP8X4),
                 rhs_scale=z_scales[:, lo:hi],
                 start=True,
@@ -176,14 +203,13 @@ def tile_picked_canddethop_none_po_kernel(
             nc.scalar.activation(s_half[t][:, lo:hi], acc, COPY, scale=0.03125)
             nc.scalar.activation(s_full[t][:, lo:hi], acc, COPY, scale=0.0625)
 
-        early = bank(4, "s_early", [P, 384])
+        early = bank(3, "s_early", [P, EARLY])
         score(early[:, 0:256], 0, 0, 256)
-        score(early[:, 256:384], 0, 256, 384)
-        empty(early[:], 0, 0, 384)
-        quantize_z(3)
-        late = bank(5, "s_late", [P, P])
-        score(late[:], 0, 384, 512)
-        empty(late[:], 0, 384, 512)
+        score(early[:, 256:EARLY], 0, 256, EARLY)
+        empty(early[:], 0, 0, EARLY)
+        late = bank(7, "s_late", [P, P])
+        score(late[:], 0, EARLY, S)
+        empty(late[:], 0, EARLY, S)
         for t, number in ((1, 6), (2, 0), (3, 1)):
             acc = bank(number, "s_acc%d" % t, [P, S])
             score(acc[:], t, 0, S)
@@ -203,22 +229,30 @@ def tile_picked_canddethop_none_po_kernel(
         o_scales = sb("o_scales", [P, S], U8)
         words_out = out_1[0].rearrange("p n t -> p (n t)").bitcast(I32)
         rounded = []
+
+        def regroup(copy, grouped, result):
+            copy(grouped[:].rearrange("p (c i t) -> p c t i", i=4, t=PACK), result[:].rearrange("p t (c i) -> p c t i", i=4))
+
         for lo, hi in OUT_CHUNKS:
             width = hi - lo
             result = sb("result%d" % lo, [P, PACK, width], F32)
             for t in range(PACK):
                 nc.vector.tensor_tensor(result[:, t, :], st_neg[t][:].indirect(entries(lists["n6"], lo, hi)), st[t][:, lo:hi], ADD)
             nc.sync.dma_start(out_rows[:, :, lo:hi], result[:])
-            grouped = sb("o_grouped%d" % lo, [P, width * PACK], BF16)
-            nc.scalar.copy(
-                grouped[:].rearrange("p (c i t) -> p c t i", i=4, t=PACK), result[:].rearrange("p t (c i) -> p c t i", i=4)
-            )
-            rounded.append(grouped)
-        for (lo, hi), grouped in zip(OUT_CHUNKS, rounded):
-            nc.vector.quantize_mx(out=o_words[:, lo:hi].bitcast(FP8X4), scales=o_scales[:, lo:hi], in_=grouped[:])
-            if hi >= 384:
-                start = 0 if hi == 384 else lo
-                nc.sync.dma_start(words_out[:, start:hi], o_words[:, start:hi].bitcast(I32))
+            rounded.append((sb("o_grouped%d" % lo, [P, width * PACK], BF16), result))
+            if hi < S:
+                regroup(nc.scalar.copy, *rounded[-1])
+
+        def quantize_out(c):
+            lo, hi = OUT_CHUNKS[c]
+            nc.vector.quantize_mx(out=o_words[:, lo:hi].bitcast(FP8X4), scales=o_scales[:, lo:hi], in_=rounded[c][0][:])
+
+        quantize_out(0)
+        regroup(nc.vector.tensor_copy, *rounded[2])
+        quantize_out(1)
+        nc.sync.dma_start(words_out[:, :EARLY], o_words[:, :EARLY].bitcast(I32))
+        quantize_out(2)
+        nc.sync.dma_start(words_out[:, EARLY:], o_words[:, EARLY:].bitcast(I32))
         for q in range(4):
             queue = nc.scalar if q % 2 == 0 else nc.sync
             queue.dma_start(out_2[0, 4 * q : 4 * q + 4, :].bitcast(I32), o_scales[32 * q : 32 * q + 4, :].bitcast(I32))

from contextlib import ExitStack

import concourse.mybir as mybir
from concourse.masks import make_identity

F32 = mybir.dt.float32
BF16 = mybir.dt.bfloat16
I32 = mybir.dt.int32
U32 = mybir.dt.uint32
U16 = mybir.dt.uint16
U8 = mybir.dt.uint8
FP8X4 = mybir.dt.float8_e4m3fn_x4
FP4X4 = mybir.dt.float4_e2m1fn_x4
MULT = mybir.AluOpType.mult
ADD = mybir.AluOpType.add
COPY = mybir.ActivationFunctionType.Copy

P = 128
PACK = 4
T = 2048
S = 512
FLOPS = 2 * 2 * 512 * 512 * 512

ST_CHUNKS = ((0, 256), (256, 512))
OUT_CHUNKS = ((0, 256), (256, 384), (384, 512))


def entries(lst, lo, hi):
    return lst[:, lo // 16 : hi // 16]


def tile_picked_canddethop_none_po_kernel(
    tc, x_words, x_scales, w1_words, w1_scales, gs, offs, n1, n2, n3, n4, cand, n5, n6, out_0, out_1, out_2
):
    nc = tc.nc
    with ExitStack() as ctx:
        keep = ctx.enter_context(tc.tile_pool(name="keep", bufs=1))
        psum = ctx.enter_context(tc.psum_pool(name="psum", bufs=1))

        def sb(name, shape, dtype, tag=None):
            return keep.tile(shape, dtype, name=name, tag=tag or name, align_bytes=64)

        def bank(number, name, shape):
            return psum.tile(shape, F32, name=name, tag="bank%d" % number)

        w_raw = sb("w_raw", [P, 2 * S], U8)
        xw = sb("xw", [P, T], I32)
        xs = sb("xs", [P, T], U8)
        ws_raw = sb("ws_raw", [P, S], U8)
        lists = {}

        def load_list(name, source):
            lists[name] = keep.tile([P, S // 16], U16, name="list_" + name)
            nc.sync.dma_start(lists[name][:], source)

        def load_scale_rows(queue, tile, source, q):
            queue.dma_start(tile[32 * q : 32 * q + 4, :].bitcast(I32), source[0, 4 * q : 4 * q + 4, :].bitcast(I32))

        nc.gpsimd.memset(xs[:].bitcast(I32), 0)
        nc.gpsimd.memset(ws_raw[:].bitcast(I32), 0)
        gain = sb("gain", [P, PACK], F32)
        load_list("offs", offs)
        nc.sync.dma_start(w_raw[:].bitcast(I32), w1_words[0].bitcast(I32))
        for q in range(4):
            load_scale_rows(nc.sync if q < 2 else nc.scalar, xs, x_scales, q)
        nc.sync.dma_start(xw[:], x_words[0].rearrange("p n t -> p (n t)").bitcast(I32))
        for q in range(4):
            load_scale_rows(nc.sync, ws_raw, w1_scales, q)
        nc.sync.dma_start(gain[:], gs.rearrange("(p t) o -> p (t o)", t=PACK))
        for name, source in (("cand", cand), ("n1", n1), ("n3", n3), ("n2", n2), ("n4", n4), ("n5", n5), ("n6", n6)):
            load_list(name, source)
        ident = sb("ident", [P, P], F32)
        make_identity(nc, ident[:])

        gain_pos = sb("gain_pos", [P, PACK], F32)
        gain_neg = sb("gain_neg", [P, PACK], F32)
        nc.scalar.activation(gain_pos[:], gain[:], COPY, scale=0.75)
        nc.scalar.activation(gain_neg[:], gain[:], COPY, scale=-0.75)

        w_dealt = sb("w_dealt", [P, 2 * S], U8)
        ws_dealt = sb("ws_dealt", [P, S], U8)
        nc.vector.tensor_copy(
            w_dealt[:].rearrange("p (t m b) -> p m t b", t=PACK, b=2), w_raw[:].rearrange("p (m t b) -> p m t b", t=PACK, b=2)
        )
        tok_w = sb("tok_w", [P, S], U32)
        tok_s = sb("tok_s", [P, S], U8)
        ws_from = ws_raw[:].rearrange("p (m t) -> p m t", t=PACK)
        ws_to = ws_dealt[:].rearrange("p (t m) -> p m t", t=PACK)
        nc.vector.tensor_copy(tok_s[:], xs[:].indirect(lists["offs"][:]))
        nc.vector.tensor_copy(tok_w[:], xw[:].bitcast(U32).indirect(lists["offs"][:]))
        nc.vector.tensor_copy(ws_to[:, :, 0], ws_from[:, :, 0])

        nc.vector.tensor_copy(ws_to[:, :, 1:], ws_from[:, :, 1:])
        cand_w = sb("cand_w", [P, S], U32)
        cand_w_dealt = sb("cand_w_dealt", [P, S], U32)
        nc.vector.tensor_copy(cand_w[:], xw[:].bitcast(U32).indirect(lists["cand"][:]))

        y_pos, y_neg, y_plain = [], [], []
        for t in range(PACK):
            acc = bank(t, "y_acc%d" % t, [P, S])
            nc.tensor.matmul_mx(
                out=acc[:],
                lhsT=w_dealt[:, 2 * P * t : 2 * P * (t + 1)].bitcast(FP4X4),
                lhsT_scale=ws_dealt[:, P * t : P * (t + 1)],
                rhs=tok_w[:].bitcast(FP8X4),
                rhs_scale=tok_s[:],
                start=True,
                stop=True,
            )
            y_pos.append(sb("y_pos%d" % t, [P, S], F32))
            y_neg.append(sb("y_neg%d" % t, [P, S], F32))
            y_plain.append(sb("y_plain%d" % t, [P, S], F32))
            nc.scalar.activation(y_pos[t][:], acc[:], COPY, scale=gain_pos[:, t : t + 1])
            nc.scalar.activation(y_neg[t][:], acc[:], COPY, scale=gain_neg[:, t : t + 1])
            nc.scalar.copy(y_plain[t][:], acc[:])

        EARLY = 3 * P
        left = sb("left", [P, EARLY], F32)
        right = sb("right", [P, EARLY], F32)
        z_words = sb("z_words", [P, S], U32)
        z_scales = sb("z_scales", [P, S], U8)

        def fetch(t, lo, hi, into):
            nc.vector.tensor_copy(into[:, : hi - lo], y_pos[t][:].indirect(entries(lists["n1"], lo, hi)))
            nc.vector.tensor_copy(right[:, : hi - lo], y_neg[t][:].indirect(entries(lists["n3"], lo, hi)))

        def multiply(t, lo, hi, fetched, first, second):
            nc.vector.tensor_tensor(first, y_plain[t][:].indirect(entries(lists["n2"], lo, hi)), fetched[:, : hi - lo], MULT)
            nc.vector.tensor_tensor(second, y_plain[t][:].indirect(entries(lists["n4"], lo, hi)), right[:, : hi - lo], MULT)

        def quantize_z(b, grouped):
            cols = slice(b * P, (b + 1) * P)
            nc.vector.quantize_mx(out=z_words[:, cols].bitcast(FP8X4), scales=z_scales[:, cols], in_=grouped[:])

        turned = [bank(4 + b, "turned%d" % b, [P, PACK, P]) for b in range(3)]
        for t in range(PACK):
            first = sb("first%d" % t, [P, EARLY], F32)
            second = sb("second%d" % t, [P, EARLY], F32)
            fetch(t, 0, EARLY, left)
            if t == 0:
                nc.vector.tensor_copy(
                    cand_w_dealt[:].bitcast(I32).rearrange("p (t m) -> p m t", t=PACK),
                    cand_w[:].bitcast(I32).rearrange("p (m t) -> p m t", t=PACK),
                )
            multiply(t, 0, EARLY, left, first[:], second[:])
            for b in range(3):
                cols = slice(b * P, (b + 1) * P)
                nc.tensor.matmul(turned[b][:, t, :], first[:, cols], ident[:], start=True, stop=False, is_transpose=True)
                nc.tensor.matmul(turned[b][:, t, :], second[:, cols], ident[:], start=False, stop=True, is_transpose=True)
        z_grouped = []
        for b in range(3):
            pairs = sb("pairs%d" % b, [P, S], BF16)
            nc.scalar.copy(
                pairs[:].rearrange("j (u p e) -> j u p e", u=2, e=2), turned[b][:].rearrange("j (u e) p -> j u p e", e=2)
            )
            back = bank(b, "back%d" % b, [P, 2, P])
            for u in range(2):
                nc.tensor.transpose(back[:, u, :], pairs[:].bitcast(F32)[:, u * P : (u + 1) * P], ident[:])
            z_grouped.append(sb("grouped%d" % b, [P, S], BF16))
            nc.scalar.copy(z_grouped[b][:].bitcast(F32).rearrange("p (j u) -> p j u", u=2), back[:].rearrange("p u j -> p j u"))

        first = sb("first_late", [P, PACK, P], F32)
        second = sb("second_late", [P, PACK, P], F32)
        for t in range(PACK - 1):
            fetch(t, EARLY, S, left)
            multiply(t, EARLY, S, left, first[:, t, :], second[:, t, :])
        cand_s = sb("cand_s", [P, S], U8, tag="y_plain2")
        cs_from = cand_s[:].rearrange("p (m t) -> p m t", t=PACK)
        cs_first = sb("cs_first", [P, P], U8)
        nc.vector.tensor_copy(cand_s[:], xs[:].indirect(lists["cand"][:]))
        for b in range(3):
            quantize_z(b, z_grouped[b])
        nc.vector.tensor_copy(cs_first[:], cs_from[:, :, 0])
        left_last = sb("left_last", [P, P], F32, tag="grouped2")
        fetch(PACK - 1, EARLY, S, left_last)
        multiply(PACK - 1, EARLY, S, left_last, first[:, PACK - 1, :], second[:, PACK - 1, :])
        grouped_late = sb("grouped3", [P, S], BF16)
        nc.vector.tensor_tensor(
            grouped_late[:].rearrange("p (c i t) -> p c t i", i=4, t=PACK),
            first[:].rearrange("p t (c i) -> p c t i", i=4),
            second[:].rearrange("p t (c i) -> p c t i", i=4),
            ADD,
        )
        quantize_z(3, grouped_late)
        cs_rest = sb("cs_rest", [P, 3 * P], U8, tag="grouped3")
        nc.vector.tensor_copy(cs_rest[:].rearrange("p (t m) -> p m t", t=3), cs_from[:, :, 1:])

        def score(acc, t, lo, hi):
            nc.tensor.matmul_mx(
                out=acc,
                lhsT=cand_w_dealt[:, P * t : P * (t + 1)].bitcast(FP8X4),
                lhsT_scale=cs_first[:] if t == 0 else cs_rest[:, P * (t - 1) : P * t],
                rhs=z_words[:, lo:hi].bitcast(FP8X4),
                rhs_scale=z_scales[:, lo:hi],
                start=True,
                stop=True,
            )

        s_half = [sb("s_half%d" % t, [P, S], F32) for t in range(PACK)]
        s_full = [sb("s_full%d" % t, [P, S], F32) for t in range(PACK)]

        def empty(acc, t, lo, hi):
            nc.scalar.activation(s_half[t][:, lo:hi], acc, COPY, scale=0.03125)
            nc.scalar.activation(s_full[t][:, lo:hi], acc, COPY, scale=0.0625)

        early = bank(3, "s_early", [P, EARLY])
        score(early[:, 0:256], 0, 0, 256)
        score(early[:, 256:EARLY], 0, 256, EARLY)
        empty(early[:], 0, 0, EARLY)
        late = bank(7, "s_late", [P, P])
        score(late[:], 0, EARLY, S)
        empty(late[:], 0, EARLY, S)
        for t, number in ((1, 6), (2, 0), (3, 1)):
            acc = bank(number, "s_acc%d" % t, [P, S])
            score(acc[:], t, 0, S)
            empty(acc[:], t, 0, S)

        st, st_neg = [], []
        for t in range(PACK):
            st.append(sb("st%d" % t, [P, S], F32))
            for lo, hi in ST_CHUNKS:
                nc.vector.tensor_tensor(st[t][:, lo:hi], s_half[t][:].indirect(entries(lists["n5"], lo, hi)), s_full[t][:, lo:hi], ADD)
        for t in range(PACK):
            st_neg.append(sb("st_neg%d" % t, [P, S], F32))
            nc.scalar.activation(st_neg[t][:], st[t][:], COPY, scale=-1.0)

        out_rows = out_0.rearrange("(p t) j -> p t j", t=PACK)
        o_words = sb("o_words", [P, S], U32)
        o_scales = sb("o_scales", [P, S], U8)
        words_out = out_1[0].rearrange("p n t -> p (n t)").bitcast(I32)
        rounded = []

        def regroup(copy, grouped, result):
            copy(grouped[:].rearrange("p (c i t) -> p c t i", i=4, t=PACK), result[:].rearrange("p t (c i) -> p c t i", i=4))

        for lo, hi in OUT_CHUNKS:
            width = hi - lo
            result = sb("result%d" % lo, [P, PACK, width], F32)
            for t in range(PACK):
                nc.vector.tensor_tensor(result[:, t, :], st_neg[t][:].indirect(entries(lists["n6"], lo, hi)), st[t][:, lo:hi], ADD)
            nc.sync.dma_start(out_rows[:, :, lo:hi], result[:])
            rounded.append((sb("o_grouped%d" % lo, [P, width * PACK], BF16), result))
            if hi < S:
                regroup(nc.scalar.copy, *rounded[-1])

        def quantize_out(c):
            lo, hi = OUT_CHUNKS[c]
            nc.vector.quantize_mx(out=o_words[:, lo:hi].bitcast(FP8X4), scales=o_scales[:, lo:hi], in_=rounded[c][0][:])

        quantize_out(0)
        regroup(nc.vector.tensor_copy, *rounded[2])
        quantize_out(1)
        nc.sync.dma_start(words_out[:, :EARLY], o_words[:, :EARLY].bitcast(I32))
        quantize_out(2)
        nc.sync.dma_start(words_out[:, EARLY:], o_words[:, EARLY:].bitcast(I32))
        for q in range(4):
            queue = nc.scalar if q % 2 == 0 else nc.sync
            queue.dma_start(out_2[0, 4 * q : 4 * q + 4, :].bitcast(I32), o_scales[32 * q : 32 * q + 4, :].bitcast(I32))
